import numpy as np
import ml_dtypes


def mxq(x, axis, fmt="e4m3"):
    dtype, down = {"e4m3": (ml_dtypes.float8_e4m3fn, 7), "e5m2": (ml_dtypes.float8_e5m2, 14)}[fmt]
    v = np.moveaxis(np.asarray(x, np.float32).astype(ml_dtypes.bfloat16).astype(np.float64), axis, -1)
    blocks = v.reshape(v.shape[:-1] + (-1, 32))
    amax = np.abs(blocks).max(-1, keepdims=True)
    byte = np.maximum(np.where(amax > 0, np.frexp(amax)[1] - 1 + 127, 0) - down, 1)
    scale = np.exp2(byte - 127.0)
    codes = (blocks / scale).astype(np.float32).astype(dtype).astype(np.float64)
    return np.moveaxis((codes * scale).reshape(v.shape), -1, axis)


WIDE = False


def mx_kscale(k):
    if not WIDE:
        return np.ones(k)
    levels = np.array([10, -10, 5, -5, 0])
    if k % 512:
        return np.exp2(np.random.permutation(np.resize(levels, k // 32))).repeat(32)
    a = np.empty((k // 512, 16))
    for p in range(k // 512):
        a[p, :8] = np.random.permutation(np.resize(levels, 8))
        for g in range(8):
            far = levels[np.abs(levels - a[p, g]) >= 10]
            a[p, g + 8] = far[np.random.randint(len(far))]
    return np.exp2(a.ravel()).repeat(32)


def f64(x):
    return np.asarray(x).astype(np.float64)


def striped(idx):
    return np.tile(idx.reshape(-1, 16).T, (8, 1)).astype(np.uint16)


def unstriped(offs):
    return offs[:16].T.reshape(-1).astype(np.int64)


def striped8(idx):
    return np.concatenate([x.reshape(-1, 16).T for x in idx]).astype(np.uint16)


def runs(offs, k):
    lists = np.stack([offs[16 * r : 16 * r + 16].T.reshape(-1) for r in range(8)]).astype(np.int64)
    return lists[np.arange(k) % 512 // 64]


def pack_weight(w):
    k, n = w.shape
    w = f64(np.asarray(w, np.float32).astype(ml_dtypes.bfloat16)).reshape(k // 32, 32, n)
    amax = np.abs(w).max(1)
    byte = np.clip(np.where(amax > 0, np.frexp(amax)[1] - 1 + 127 - 7, 1), 1, 254)
    scaled = (w * np.exp2(127.0 - byte)[:, None, :]).reshape(k, n).astype(np.float32)
    words = np.ascontiguousarray(scaled.reshape(k // 512, 128, 4, n).transpose(0, 1, 3, 2)).astype(ml_dtypes.float8_e4m3fn).view(np.uint8)
    return words, np.ascontiguousarray(byte.astype(np.uint8).reshape(k // 512, 16, n))


def unpack_weight(words, scales):
    g, p, n, _ = words.shape
    vals = np.ascontiguousarray(words).view(ml_dtypes.float8_e4m3fn).astype(np.float64) * np.repeat(np.exp2(scales.astype(np.float64) - 127.0), 8, axis=1)[..., None]
    return vals.transpose(0, 1, 3, 2).reshape(g * 512, n)


def relu(v):
    return np.maximum(v, 0.0)


K, T, S, V, H = 512, 2048, 512, 256, 512


def setup_inputs():
    n = np.random.standard_normal
    s = mx_kscale(K)[:, None]
    u = mx_kscale(S)
    packed_xT = pack_weight(n((K, T)) * s)
    return {
        "x_words": packed_xT[0],
        "x_scales": packed_xT[1],
        "w1": (n((K, H)) / np.sqrt(K) / s).astype(np.float32),
        "w2": (n((K, H)) / np.sqrt(K) / s).astype(np.float32),
        "ga": (np.random.uniform(0.5, 1.5, (H, 1)) * u[:, None]).astype(np.float32),
        "gb": (np.random.uniform(0.5, 1.5, (H, 1)) / u[:, None]).astype(np.float32),
        "offs": striped8(np.random.randint(0, T, (8, S))),
        "two": striped(np.random.permutation(T)[:V]),
        "n1": striped8(np.stack([np.random.permutation(S) for _ in range(8)])),
        "n2": striped8(np.stack([np.random.permutation(S) for _ in range(8)])),
        "n3": striped(np.random.permutation(V)),
        "n4": striped(np.random.permutation(V)),
        "n5": striped(np.random.permutation(V)),
    }


def reference(x_words, x_scales, w1, w2, ga, gb, offs, two, n1, n2, n3, n4, n5):
    xq = unpack_weight(x_words, x_scales)[np.arange(K)[:, None], runs(offs, K)]
    a = mxq(f64(w1), 0, "e4m3").T @ xq
    st = a + 0.5 * (a[np.arange(H)[:, None], runs(n1, H)])
    z = f64(ga) * (st - (st[np.arange(H)[:, None], runs(n2, H)]))
    x_two = unpack_weight(x_words, x_scales)[:, unstriped(two)]
    b = mxq(f64(w2), 0, "e4m3").T @ x_two
    rl = relu(b)
    ds = np.zeros((H, V))
    ds[:, unstriped(n3)] = rl
    z2 = f64(gb) * (ds - (0.5 * b))
    s = 0.0625 * ((mxq(z, 0, "e4m3").T @ mxq(z2, 0, "e4m3")))
    return s[:, unstriped(n4)] - s[:, unstriped(n5)]

@@ -1,0 +1,177 @@
+from contextlib import ExitStack
+
+import concourse.mybir as mybir
+
+F32 = mybir.dt.float32
+BF16 = mybir.dt.bfloat16
+I32 = mybir.dt.int32
+U32 = mybir.dt.uint32
+U16 = mybir.dt.uint16
+U8 = mybir.dt.uint8
+FP8X4 = mybir.dt.float8_e4m3fn_x4
+ALU = mybir.AluOpType
+COPY = mybir.ActivationFunctionType.Copy
+
+P = 128
+PACK = 4
+T, S, V, H = 2048, 512, 256, 512
+HALF = S // 2
+SPARE = 16
+
+FLOPS = 2 * 512 * (H * S + H * V + S * V)
+
+
+def tile_picked_hkqhopsendgap_none_p_kernel(
+    tc, x_words, x_scales, w1, w2, ga, gb, offs, two, n1, n2, n3, n4, n5, out
+):
+    nc = tc.nc
+    with ExitStack() as ctx:
+        keep = ctx.enter_context(tc.tile_pool(name="keep", bufs=1))
+        psum = ctx.enter_context(tc.psum_pool(name="psum", bufs=1))
+
+        def sb(name, shape, dtype):
+            return keep.tile(shape, dtype, name=name, align_bytes=64)
+
+        def load_list(name, src):
+            tile = sb(name, [P, src.shape[1]], U16)
+            nc.sync.dma_start(tile[:], src)
+            return tile
+
+        def mx(acc, lhs, lhs_scale, rhs, rhs_scale):
+            nc.tensor.matmul_mx(out=acc, lhsT=lhs.bitcast(FP8X4), lhsT_scale=lhs_scale,
+                                rhs=rhs.bitcast(FP8X4), rhs_scale=rhs_scale, start=True, stop=True)
+
+        def load_weight_half(name, w, h):
+            raw = sb(name, [P, PACK, HALF], F32)
+            nc.sync.dma_start(out=raw[:], in_=w.rearrange("(p j) c -> p j c", j=PACK)[:, :, h * HALF:(h + 1) * HALF])
+            return raw
+
+        def deal(copy, grouped, raw, h):
+            m = HALF // PACK
+            copy(out=grouped[:].rearrange("p (t m j) -> p m j t", t=PACK, j=PACK)[:, h * m:(h + 1) * m],
+                 in_=raw[:].rearrange("p j (m t) -> p m j t", t=PACK))
+
+        x_s = sb("x_s", [P, T], U8)
+        nc.gpsimd.memset(x_s[:].bitcast(I32), 0)
+        nc.scalar.dma_start(out=x_s[0:P:8, :].bitcast(I32), in_=x_scales[0].bitcast(I32))
+        offs_t = load_list("offs_t", offs)
+        two_t = load_list("two_t", two)
+        gb_t = sb("gb_t", [P, PACK], F32)
+        nc.sync.dma_start(out=gb_t[:], in_=gb.rearrange("(p t) o -> p (t o)", t=PACK))
+        x_w = sb("x_w", [P, T], U32)
+        nc.sync.dma_start(out=x_w[:].bitcast(I32), in_=x_words[0].rearrange("p n t -> p (n t)").bitcast(I32))
+        n1_t = load_list("n1_t", n1)
+        n2_t = load_list("n2_t", n2)
+        n3_t = load_list("n3_t", n3)
+        w1_raw = [load_weight_half("w1_raw%d" % h, w1, h) for h in range(2)]
+        ga_t = sb("ga_t", [P, PACK], F32)
+        nc.sync.dma_start(out=ga_t[:], in_=ga.rearrange("(p t) o -> p (t o)", t=PACK))
+        n4_t = load_list("n4_t", n4)
+        n5_t = load_list("n5_t", n5)
+        gb_half = sb("gb_half", [P, PACK], F32)
+        nc.scalar.activation(gb_half[:], gb_t[:], COPY, scale=-0.5)
+
+        plane = sb("plane", [P, S + V], U8)
+        picked_s = sb("picked_s", [P, S + V], U8)
+        nc.vector.tensor_copy(picked_s[:, 0:S], x_s[:].indirect(offs_t[:]))
+        nc.vector.tensor_copy(picked_s[:, S:S + V], x_s[:].indirect(two_t[:]))
+        nc.vector.tensor_copy(plane[:].bitcast(I32), picked_s[:].bitcast(I32))
+        for i in range(1, 4):
+            nc.scalar.dma_start(out=plane[i:P:32, :].bitcast(I32), in_=picked_s[8 * i:P:32, :].bitcast(I32))
+        w2_raw = sb("picked_s", [P, PACK, H], F32)
+        nc.sync.dma_start(out=w2_raw[:], in_=w2.rearrange("(p j) c -> p j c", j=PACK))
+
+        xa = sb("xa", [P, S], U32)
+        nc.vector.tensor_copy(xa[:], x_w[:].indirect(offs_t[:]))
+        w1_bf = sb("w1_bf", [P, PACK * H], BF16)
+        deal(nc.vector.tensor_copy, w1_bf, w1_raw[0], 0)
+        xb = sb("xb", [P, V], U32)
+        nc.vector.tensor_copy(xb[:], x_w[:].indirect(two_t[:]))
+        deal(nc.vector.tensor_copy, w1_bf, w1_raw[1], 1)
+        w1_q = sb("w1_q", [P, H], U32)
+        w1_s = sb("w1_s", [P, H], U8)
+
+        a_ps = [psum.tile([P, S], F32, name="a_ps%d" % t) for t in range(PACK)]
+        a_sb = [sb("a_sb%d" % t, [P, S], F32) for t in range(PACK)]
+        st = [sb("st%d" % t, [P, S], F32) for t in range(PACK)]
+        twin = [sb("twin%d" % t, [P, S], F32) for t in range(PACK)]
+        hop = [sb("hop%d" % h, [P, PACK, HALF], F32) for h in range(2)]
+        back = [sb("back%d" % h, [P, PACK, HALF], F32) for h in range(2)]
+        for t in range(PACK):
+            cols = slice(t * P, (t + 1) * P)
+            nc.vector.quantize_mx(out=w1_q[:, cols].bitcast(FP8X4), scales=w1_s[:, cols],
+                                  in_=w1_bf[:, t * H:(t + 1) * H])
+            mx(a_ps[t][:], w1_q[:, cols], w1_s[:, cols], xa[:], plane[:, 0:S])
+        for t in range(PACK):
+            if t == 1:
+                nc.vector.tensor_scalar(a_sb[t][:], a_ps[t][:], ga_t[:, t:t + 1], None, ALU.mult)
+            else:
+                nc.scalar.activation(a_sb[t][:], a_ps[t][:], COPY, scale=ga_t[:, t:t + 1])
+            for h in range(2):
+                nc.scalar.activation(hop[h][:, t, :], a_sb[t][:].indirect(n1_t[:, 16 * h:16 * h + 16]), COPY, scale=0.5)
+
+        w2_bf = sb("w2_bf", [P, PACK * H], BF16)
+        nc.vector.tensor_copy(out=w2_bf[:].rearrange("p (t m j) -> p m j t", t=PACK, j=PACK),
+                              in_=w2_raw[:].rearrange("p j (m t) -> p m j t", t=PACK))
+        w2_q = sb("w2_q", [P, H], U32)
+        w2_s = sb("w2_s", [P, H], U8)
+        nc.vector.quantize_mx(out=w2_q[:].bitcast(FP8X4), scales=w2_s[:], in_=w2_bf[:])
+        b_ps = [psum.tile([P, 2, V], F32, name="b_ps%d" % u) for u in range(2)]
+        for t in range(PACK):
+            cols = slice(t * P, (t + 1) * P)
+            mx(b_ps[t // 2][:, t % 2, :], w2_q[:, cols], w2_s[:, cols], xb[:], plane[:, S:S + V])
+        rl = [sb("rl%d" % t, [P, V], F32) for t in range(PACK)]
+        ds = [sb("ds%d" % t, [P, 2 * V], F32) for t in range(PACK)]
+        for t in range(PACK):
+            nc.vector.tensor_scalar(rl[t][:], b_ps[t // 2][:, t % 2, :], 0.0, gb_t[:, t:t + 1], ALU.max, ALU.mult)
+            nc.scalar.activation(ds[t][:].indirect(n3_t[:]), rl[t][:], COPY)
+
+        for t in range(PACK):
+            for h in range(2):
+                cols = slice(h * HALF, (h + 1) * HALF)
+                nc.vector.tensor_tensor(st[t][:, cols], a_sb[t][:, cols], hop[h][:, t, :], ALU.add)
+            nc.sync.dma_start(out=twin[t][:], in_=st[t][:])
+        for t in range(PACK):
+            nc.vector.tensor_tensor(back[0][:, t, :], st[t][:].indirect(n2_t[:, 0:16]), twin[t][:, 0:HALF], ALU.subtract)
+
+        z_bf = [sb("z_bf%d" % h, [P, PACK * HALF], BF16) for h in range(2)]
+        z_q = [sb("z_q%d" % h, [P, HALF], U32) for h in range(2)]
+        z_s = [sb("z_s%d" % h, [P, HALF], U8) for h in range(2)]
+
+        def make_z(h):
+            nc.vector.tensor_copy(out=z_bf[h][:].rearrange("p (c i t) -> p c t i", i=4, t=PACK),
+                                  in_=back[h][:].rearrange("p t (c i) -> p c t i", i=4))
+
+        def quant_z(h):
+            nc.vector.quantize_mx(out=z_q[h][:].bitcast(FP8X4), scales=z_s[h][:], in_=z_bf[h][:])
+
+        make_z(0)
+        for t in range(PACK):
+            nc.vector.tensor_tensor(back[1][:, t, :], st[t][:].indirect(n2_t[:, 16:32]), twin[t][:, HALF:S], ALU.subtract)
+        quant_z(0)
+
+        z2 = sb("twin%d" % (PACK - 1), [P, PACK, V], F32)
+        for t in range(PACK):
+            nc.vector.scalar_tensor_tensor(z2[:, t, :], b_ps[t // 2][:, t % 2, :], gb_half[:, t:t + 1], ds[t][:, 0:V],
+                                           ALU.mult, ALU.add)
+        z2_bf = sb("z2_bf", [P, PACK * V], BF16)
+        nc.vector.tensor_copy(out=z2_bf[:].rearrange("p (c i t) -> p c t i", i=4, t=PACK),
+                              in_=z2[:].rearrange("p t (c i) -> p c t i", i=4))
+        make_z(1)
+        z2_q = sb("z2_q", [P, V], U32)
+        z2_s = sb("z2_s", [P, V], U8)
+        nc.vector.quantize_mx(out=z2_q[:].bitcast(FP8X4), scales=z2_s[:], in_=z2_bf[:])
+        quant_z(1)
+
+        for c in range(4):
+            cols = slice((c % 2) * P, (c % 2 + 1) * P)
+            s_ps = psum.tile([P, V], F32, name="s_ps", bufs=2)
+            mx(s_ps[:], z_q[c // 2][:, cols], z_s[c // 2][:, cols], z2_q[:], z2_s[:])
+            s_sb = sb("s_sb%d" % c, [P, V + SPARE], F32)
+            nc.gpsimd.memset(s_sb[:, V:V + SPARE], 0.0)
+            nc.scalar.activation(s_sb[:, 0:V], s_ps[:], COPY, scale=-0.0625)
+            less = sb("less%d" % c, [P, V], F32)
+            nc.scalar.activation(less[:], s_sb[:].indirect(n5_t[:]), COPY, scale=-1.0)
+            res = sb("res%d" % c, [P, V], F32)
+            nc.vector.tensor_tensor(res[:], s_sb[:].indirect(n4_t[:]), less[:], ALU.add)
+            nc.sync.dma_start(out=out[c * P:(c + 1) * P, :], in_=res[:])

@@ -41,15 +41,14 @@ def tile_picked_hkqhopsendgap_none_p_kernel(
             nc.tensor.matmul_mx(out=acc, lhsT=lhs.bitcast(FP8X4), lhsT_scale=lhs_scale,
                                 rhs=rhs.bitcast(FP8X4), rhs_scale=rhs_scale, start=True, stop=True)
 
-        def load_weight_half(name, w, h):
-            raw = sb(name, [P, PACK, HALF], F32)
-            nc.sync.dma_start(out=raw[:], in_=w.rearrange("(p j) c -> p j c", j=PACK)[:, :, h * HALF:(h + 1) * HALF])
+        def load_weight(w):
+            raw = sb("w_raw", [P, PACK, H], F32)
+            nc.sync.dma_start(out=raw[:], in_=w.rearrange("(p j) c -> p j c", j=PACK))
             return raw
 
-        def deal(copy, grouped, raw, h):
-            m = HALF // PACK
-            copy(out=grouped[:].rearrange("p (t m j) -> p m j t", t=PACK, j=PACK)[:, h * m:(h + 1) * m],
-                 in_=raw[:].rearrange("p j (m t) -> p m j t", t=PACK))
+        def deal(grouped, raw):
+            nc.vector.tensor_copy(out=grouped[:].rearrange("p (t m j) -> p m j t", t=PACK, j=PACK),
+                                  in_=raw[:].rearrange("p j (m t) -> p m j t", t=PACK))
 
         x_s = sb("x_s", [P, T], U8)
         nc.gpsimd.memset(x_s[:].bitcast(I32), 0)
@@ -58,12 +57,12 @@ def tile_picked_hkqhopsendgap_none_p_kernel(
         two_t = load_list("two_t", two)
         gb_t = sb("gb_t", [P, PACK], F32)
         nc.sync.dma_start(out=gb_t[:], in_=gb.rearrange("(p t) o -> p (t o)", t=PACK))
-        x_w = sb("x_w", [P, T], U32)
-        nc.sync.dma_start(out=x_w[:].bitcast(I32), in_=x_words[0].rearrange("p n t -> p (n t)").bitcast(I32))
         n1_t = load_list("n1_t", n1)
         n2_t = load_list("n2_t", n2)
         n3_t = load_list("n3_t", n3)
-        w1_raw = [load_weight_half("w1_raw%d" % h, w1, h) for h in range(2)]
+        w1_raw = load_weight(w1)
+        x_w = sb("x_w", [P, T], U32)
+        nc.sync.dma_start(out=x_w[:].bitcast(I32), in_=x_words[0].rearrange("p n t -> p (n t)").bitcast(I32))
         ga_t = sb("ga_t", [P, PACK], F32)
         nc.sync.dma_start(out=ga_t[:], in_=ga.rearrange("(p t) o -> p (t o)", t=PACK))
         n4_t = load_list("n4_t", n4)
@@ -78,61 +77,70 @@ def tile_picked_hkqhopsendgap_none_p_kernel(
         nc.vector.tensor_copy(plane[:].bitcast(I32), picked_s[:].bitcast(I32))
         for i in range(1, 4):
             nc.scalar.dma_start(out=plane[i:P:32, :].bitcast(I32), in_=picked_s[8 * i:P:32, :].bitcast(I32))
-        w2_raw = sb("picked_s", [P, PACK, H], F32)
-        nc.sync.dma_start(out=w2_raw[:], in_=w2.rearrange("(p j) c -> p j c", j=PACK))
 
-        xa = sb("xa", [P, S], U32)
-        nc.vector.tensor_copy(xa[:], x_w[:].indirect(offs_t[:]))
         w1_bf = sb("w1_bf", [P, PACK * H], BF16)
-        deal(nc.vector.tensor_copy, w1_bf, w1_raw[0], 0)
-        xb = sb("xb", [P, V], U32)
-        nc.vector.tensor_copy(xb[:], x_w[:].indirect(two_t[:]))
-        deal(nc.vector.tensor_copy, w1_bf, w1_raw[1], 1)
+        deal(w1_bf, w1_raw)
+        w2_raw = load_weight(w2)
         w1_q = sb("w1_q", [P, H], U32)
         w1_s = sb("w1_s", [P, H], U8)
+        nc.vector.quantize_mx(out=w1_q[:].bitcast(FP8X4), scales=w1_s[:], in_=w1_bf[:])
+        xa = [sb("xa%d" % h, [P, HALF], U32) for h in range(2)]
+        for h in range(2):
+            nc.vector.tensor_copy(xa[h][:], x_w[:].indirect(offs_t[:, 16 * h:16 * h + 16]))
+        xb = sb("xb", [P, V], U32)
+        nc.vector.tensor_copy(xb[:], x_w[:].indirect(two_t[:]))
 
-        a_ps = [psum.tile([P, S], F32, name="a_ps%d" % t) for t in range(PACK)]
+        def bank(n, width):
+            return psum.tile([P, width], F32, name="bank%d" % n)
+
+        a_first = [bank(h, HALF) for h in range(2)]
+        a_rest = [bank(1 + t, S) for t in range(1, PACK)]
         a_sb = [sb("a_sb%d" % t, [P, S], F32) for t in range(PACK)]
-        st = [sb("st%d" % t, [P, S], F32) for t in range(PACK)]
-        twin = [sb("twin%d" % t, [P, S], F32) for t in range(PACK)]
-        hop = [sb("hop%d" % h, [P, PACK, HALF], F32) for h in range(2)]
+        hop = [sb("hop%d" % t, [P, S], F32) for t in range(PACK)]
         back = [sb("back%d" % h, [P, PACK, HALF], F32) for h in range(2)]
-        for t in range(PACK):
-            cols = slice(t * P, (t + 1) * P)
-            nc.vector.quantize_mx(out=w1_q[:, cols].bitcast(FP8X4), scales=w1_s[:, cols],
-                                  in_=w1_bf[:, t * H:(t + 1) * H])
-            mx(a_ps[t][:], w1_q[:, cols], w1_s[:, cols], xa[:], plane[:, 0:S])
-        for t in range(PACK):
-            if t == 1:
-                nc.vector.tensor_scalar(a_sb[t][:], a_ps[t][:], ga_t[:, t:t + 1], None, ALU.mult)
-            else:
-                nc.scalar.activation(a_sb[t][:], a_ps[t][:], COPY, scale=ga_t[:, t:t + 1])
+        for pair in range(2):
             for h in range(2):
-                nc.scalar.activation(hop[h][:, t, :], a_sb[t][:].indirect(n1_t[:, 16 * h:16 * h + 16]), COPY, scale=0.5)
+                half = slice(h * HALF, (h + 1) * HALF)
+                for t in (2 * pair, 2 * pair + 1):
+                    cols = slice(t * P, (t + 1) * P)
+                    acc = a_first[h][:] if t == 0 else a_rest[t - 1][:, half]
+                    mx(acc, w1_q[:, cols], w1_s[:, cols], xa[h][:], plane[:, half])
+        for t in range(PACK):
+            if t == 0:
+                for h in range(2):
+                    nc.scalar.activation(a_sb[0][:, h * HALF:(h + 1) * HALF], a_first[h][:], COPY, scale=ga_t[:, 0:1])
+            elif t == PACK - 1:
+                nc.scalar.activation(a_sb[t][:], a_rest[t - 1][:], COPY, scale=ga_t[:, t:t + 1])
+            else:
+                nc.vector.tensor_scalar(a_sb[t][:], a_rest[t - 1][:], ga_t[:, t:t + 1], None, ALU.mult)
+            for h in range(2):
+                nc.scalar.activation(hop[t][:, h * HALF:(h + 1) * HALF], a_sb[t][:].indirect(n1_t[:, 16 * h:16 * h + 16]),
+                                     COPY, scale=0.5)
 
         w2_bf = sb("w2_bf", [P, PACK * H], BF16)
-        nc.vector.tensor_copy(out=w2_bf[:].rearrange("p (t m j) -> p m j t", t=PACK, j=PACK),
-                              in_=w2_raw[:].rearrange("p j (m t) -> p m j t", t=PACK))
+        deal(w2_bf, w2_raw)
         w2_q = sb("w2_q", [P, H], U32)
         w2_s = sb("w2_s", [P, H], U8)
         nc.vector.quantize_mx(out=w2_q[:].bitcast(FP8X4), scales=w2_s[:], in_=w2_bf[:])
-        b_ps = [psum.tile([P, 2, V], F32, name="b_ps%d" % u) for u in range(2)]
+        b_ps = [bank((5 + t) % 8, V) for t in range(PACK)]
         for t in range(PACK):
             cols = slice(t * P, (t + 1) * P)
-            mx(b_ps[t // 2][:, t % 2, :], w2_q[:, cols], w2_s[:, cols], xb[:], plane[:, S:S + V])
+            mx(b_ps[t][:], w2_q[:, cols], w2_s[:, cols], xb[:], plane[:, S:S + V])
+        st = [sb(name, [P, S], F32) for name in ("w_raw", "w2_bf", "xb", "w2_q")]
         rl = [sb("rl%d" % t, [P, V], F32) for t in range(PACK)]
         ds = [sb("ds%d" % t, [P, 2 * V], F32) for t in range(PACK)]
         for t in range(PACK):
-            nc.vector.tensor_scalar(rl[t][:], b_ps[t // 2][:, t % 2, :], 0.0, gb_t[:, t:t + 1], ALU.max, ALU.mult)
+            nc.vector.tensor_scalar(rl[t][:], b_ps[t][:], 0.0, gb_t[:, t:t + 1], ALU.max, ALU.mult)
             nc.scalar.activation(ds[t][:].indirect(n3_t[:]), rl[t][:], COPY)
 
+        twin = [sb("twin%d" % t, [P, S if t < 2 else HALF], F32) for t in range(PACK)]
         for t in range(PACK):
-            for h in range(2):
-                cols = slice(h * HALF, (h + 1) * HALF)
-                nc.vector.tensor_tensor(st[t][:, cols], a_sb[t][:, cols], hop[h][:, t, :], ALU.add)
-            nc.sync.dma_start(out=twin[t][:], in_=st[t][:])
-        for t in range(PACK):
-            nc.vector.tensor_tensor(back[0][:, t, :], st[t][:].indirect(n2_t[:, 0:16]), twin[t][:, 0:HALF], ALU.subtract)
+            nc.vector.tensor_tensor(st[t][:], a_sb[t][:], hop[t][:], ALU.add)
+            nc.sync.dma_start(out=twin[t][:], in_=st[t][:, 0:twin[t].shape[1]])
+
+        def fetch_back(t, h):
+            nc.vector.tensor_tensor(back[h][:, t, :], st[t][:].indirect(n2_t[:, 16 * h:16 * h + 16]),
+                                    twin[t][:, h * HALF:(h + 1) * HALF], ALU.subtract)
 
         z_bf = [sb("z_bf%d" % h, [P, PACK * HALF], BF16) for h in range(2)]
         z_q = [sb("z_q%d" % h, [P, HALF], U32) for h in range(2)]
@@ -145,27 +153,35 @@ def tile_picked_hkqhopsendgap_none_p_kernel(
         def quant_z(h):
             nc.vector.quantize_mx(out=z_q[h][:].bitcast(FP8X4), scales=z_s[h][:], in_=z_bf[h][:])
 
+        for h in range(2):
+            for t in range(2):
+                fetch_back(t, h)
+        for t in range(2, PACK):
+            fetch_back(t, 0)
         make_z(0)
-        for t in range(PACK):
-            nc.vector.tensor_tensor(back[1][:, t, :], st[t][:].indirect(n2_t[:, 16:32]), twin[t][:, HALF:S], ALU.subtract)
         quant_z(0)
 
-        z2 = sb("twin%d" % (PACK - 1), [P, PACK, V], F32)
+        z2 = sb("back0", [P, PACK, V], F32)
         for t in range(PACK):
-            nc.vector.scalar_tensor_tensor(z2[:, t, :], b_ps[t // 2][:, t % 2, :], gb_half[:, t:t + 1], ds[t][:, 0:V],
+            nc.vector.scalar_tensor_tensor(z2[:, t, :], b_ps[t][:], gb_half[:, t:t + 1], ds[t][:, 0:V],
                                            ALU.mult, ALU.add)
+        far = [sb("ds%d" % t, [P, HALF], F32) for t in range(2, PACK)]
+        for t in range(2, PACK):
+            nc.scalar.activation(far[t - 2][:], st[t][:].indirect(n2_t[:, 16:32]), COPY)
         z2_bf = sb("z2_bf", [P, PACK * V], BF16)
         nc.vector.tensor_copy(out=z2_bf[:].rearrange("p (c i t) -> p c t i", i=4, t=PACK),
                               in_=z2[:].rearrange("p t (c i) -> p c t i", i=4))
-        make_z(1)
         z2_q = sb("z2_q", [P, V], U32)
         z2_s = sb("z2_s", [P, V], U8)
         nc.vector.quantize_mx(out=z2_q[:].bitcast(FP8X4), scales=z2_s[:], in_=z2_bf[:])
+        for t in range(2, PACK):
+            nc.vector.tensor_tensor(back[1][:, t, :], far[t - 2][:], st[t][:, HALF:S], ALU.subtract)
+        make_z(1)
         quant_z(1)
 
         for c in range(4):
             cols = slice((c % 2) * P, (c % 2 + 1) * P)
-            s_ps = psum.tile([P, V], F32, name="s_ps", bufs=2)
+            s_ps = bank(1 + c, V)
             mx(s_ps[:], z_q[c // 2][:, cols], z_s[c // 2][:, cols], z2_q[:], z2_s[:])
             s_sb = sb("s_sb%d" % c, [P, V + SPARE], F32)
             nc.gpsimd.memset(s_sb[:, V:V + SPARE], 0.0)

from contextlib import ExitStack

import concourse.mybir as mybir

F32 = mybir.dt.float32
BF16 = mybir.dt.bfloat16
I32 = mybir.dt.int32
U32 = mybir.dt.uint32
U16 = mybir.dt.uint16
U8 = mybir.dt.uint8
FP8X4 = mybir.dt.float8_e4m3fn_x4
ALU = mybir.AluOpType
COPY = mybir.ActivationFunctionType.Copy

P = 128
PACK = 4
T, S, V, H = 2048, 512, 256, 512
HALF = S // 2
SPARE = 16

FLOPS = 2 * 512 * (H * S + H * V + S * V)


def tile_picked_hkqhopsendgap_none_p_kernel(
    tc, x_words, x_scales, w1, w2, ga, gb, offs, two, n1, n2, n3, n4, n5, out
):
    nc = tc.nc
    with ExitStack() as ctx:
        keep = ctx.enter_context(tc.tile_pool(name="keep", bufs=1))
        psum = ctx.enter_context(tc.psum_pool(name="psum", bufs=1))

        def sb(name, shape, dtype):
            return keep.tile(shape, dtype, name=name, align_bytes=64)

        def load_list(name, src):
            tile = sb(name, [P, src.shape[1]], U16)
            nc.sync.dma_start(tile[:], src)
            return tile

        def mx(acc, lhs, lhs_scale, rhs, rhs_scale):
            nc.tensor.matmul_mx(out=acc, lhsT=lhs.bitcast(FP8X4), lhsT_scale=lhs_scale,
                                rhs=rhs.bitcast(FP8X4), rhs_scale=rhs_scale, start=True, stop=True)

        def load_weight(w):
            raw = sb("w_raw", [P, PACK, H], F32)
            nc.sync.dma_start(out=raw[:], in_=w.rearrange("(p j) c -> p j c", j=PACK))
            return raw

        def deal(grouped, raw):
            nc.vector.tensor_copy(out=grouped[:].rearrange("p (t m j) -> p m j t", t=PACK, j=PACK),
                                  in_=raw[:].rearrange("p j (m t) -> p m j t", t=PACK))

        x_s = sb("x_s", [P, T], U8)
        nc.gpsimd.memset(x_s[:].bitcast(I32), 0)
        nc.scalar.dma_start(out=x_s[0:P:8, :].bitcast(I32), in_=x_scales[0].bitcast(I32))
        offs_t = load_list("offs_t", offs)
        two_t = load_list("two_t", two)
        gb_t = sb("gb_t", [P, PACK], F32)
        nc.sync.dma_start(out=gb_t[:], in_=gb.rearrange("(p t) o -> p (t o)", t=PACK))
        n1_t = load_list("n1_t", n1)
        n2_t = load_list("n2_t", n2)
        n3_t = load_list("n3_t", n3)
        w1_raw = load_weight(w1)
        x_w = sb("x_w", [P, T], U32)
        nc.sync.dma_start(out=x_w[:].bitcast(I32), in_=x_words[0].rearrange("p n t -> p (n t)").bitcast(I32))
        ga_t = sb("ga_t", [P, PACK], F32)
        nc.sync.dma_start(out=ga_t[:], in_=ga.rearrange("(p t) o -> p (t o)", t=PACK))
        n4_t = load_list("n4_t", n4)
        n5_t = load_list("n5_t", n5)
        gb_half = sb("gb_half", [P, PACK], F32)
        nc.scalar.activation(gb_half[:], gb_t[:], COPY, scale=-0.5)

        plane = sb("plane", [P, S + V], U8)
        picked_s = sb("picked_s", [P, S + V], U8)
        nc.vector.tensor_copy(picked_s[:, 0:S], x_s[:].indirect(offs_t[:]))
        nc.vector.tensor_copy(picked_s[:, S:S + V], x_s[:].indirect(two_t[:]))
        nc.vector.tensor_copy(plane[:].bitcast(I32), picked_s[:].bitcast(I32))
        for i in range(1, 4):
            nc.scalar.dma_start(out=plane[i:P:32, :].bitcast(I32), in_=picked_s[8 * i:P:32, :].bitcast(I32))

        w1_bf = sb("w1_bf", [P, PACK * H], BF16)
        deal(w1_bf, w1_raw)
        w2_raw = load_weight(w2)
        w1_q = sb("w1_q", [P, H], U32)
        w1_s = sb("w1_s", [P, H], U8)
        nc.vector.quantize_mx(out=w1_q[:].bitcast(FP8X4), scales=w1_s[:], in_=w1_bf[:])
        xa = [sb("xa%d" % h, [P, HALF], U32) for h in range(2)]
        for h in range(2):
            nc.vector.tensor_copy(xa[h][:], x_w[:].indirect(offs_t[:, 16 * h:16 * h + 16]))
        xb = sb("xb", [P, V], U32)
        nc.vector.tensor_copy(xb[:], x_w[:].indirect(two_t[:]))

        def bank(n, width):
            return psum.tile([P, width], F32, name="bank%d" % n)

        a_first = [bank(h, HALF) for h in range(2)]
        a_rest = [bank(1 + t, S) for t in range(1, PACK)]
        a_sb = [sb("a_sb%d" % t, [P, S], F32) for t in range(PACK)]
        hop = [sb("hop%d" % t, [P, S], F32) for t in range(PACK)]
        back = [sb("back%d" % h, [P, PACK, HALF], F32) for h in range(2)]
        for pair in range(2):
            for h in range(2):
                half = slice(h * HALF, (h + 1) * HALF)
                for t in (2 * pair, 2 * pair + 1):
                    cols = slice(t * P, (t + 1) * P)
                    acc = a_first[h][:] if t == 0 else a_rest[t - 1][:, half]
                    mx(acc, w1_q[:, cols], w1_s[:, cols], xa[h][:], plane[:, half])
        for t in range(PACK):
            if t == 0:
                for h in range(2):
                    nc.scalar.activation(a_sb[0][:, h * HALF:(h + 1) * HALF], a_first[h][:], COPY, scale=ga_t[:, 0:1])
            elif t == PACK - 1:
                nc.scalar.activation(a_sb[t][:], a_rest[t - 1][:], COPY, scale=ga_t[:, t:t + 1])
            else:
                nc.vector.tensor_scalar(a_sb[t][:], a_rest[t - 1][:], ga_t[:, t:t + 1], None, ALU.mult)
            for h in range(2):
                nc.scalar.activation(hop[t][:, h * HALF:(h + 1) * HALF], a_sb[t][:].indirect(n1_t[:, 16 * h:16 * h + 16]),
                                     COPY, scale=0.5)

        w2_bf = sb("w2_bf", [P, PACK * H], BF16)
        deal(w2_bf, w2_raw)
        w2_q = sb("w2_q", [P, H], U32)
        w2_s = sb("w2_s", [P, H], U8)
        nc.vector.quantize_mx(out=w2_q[:].bitcast(FP8X4), scales=w2_s[:], in_=w2_bf[:])
        b_ps = [bank((5 + t) % 8, V) for t in range(PACK)]
        for t in range(PACK):
            cols = slice(t * P, (t + 1) * P)
            mx(b_ps[t][:], w2_q[:, cols], w2_s[:, cols], xb[:], plane[:, S:S + V])
        st = [sb(name, [P, S], F32) for name in ("w_raw", "w2_bf", "xb", "w2_q")]
        rl = [sb("rl%d" % t, [P, V], F32) for t in range(PACK)]
        ds = [sb("ds%d" % t, [P, 2 * V], F32) for t in range(PACK)]
        for t in range(PACK):
            nc.vector.tensor_scalar(rl[t][:], b_ps[t][:], 0.0, gb_t[:, t:t + 1], ALU.max, ALU.mult)
            nc.scalar.activation(ds[t][:].indirect(n3_t[:]), rl[t][:], COPY)

        twin = [sb("twin%d" % t, [P, S if t < 2 else HALF], F32) for t in range(PACK)]
        for t in range(PACK):
            nc.vector.tensor_tensor(st[t][:], a_sb[t][:], hop[t][:], ALU.add)
            nc.sync.dma_start(out=twin[t][:], in_=st[t][:, 0:twin[t].shape[1]])

        def fetch_back(t, h):
            nc.vector.tensor_tensor(back[h][:, t, :], st[t][:].indirect(n2_t[:, 16 * h:16 * h + 16]),
                                    twin[t][:, h * HALF:(h + 1) * HALF], ALU.subtract)

        z_bf = [sb("z_bf%d" % h, [P, PACK * HALF], BF16) for h in range(2)]
        z_q = [sb("z_q%d" % h, [P, HALF], U32) for h in range(2)]
        z_s = [sb("z_s%d" % h, [P, HALF], U8) for h in range(2)]

        def make_z(h):
            nc.vector.tensor_copy(out=z_bf[h][:].rearrange("p (c i t) -> p c t i", i=4, t=PACK),
                                  in_=back[h][:].rearrange("p t (c i) -> p c t i", i=4))

        def quant_z(h):
            nc.vector.quantize_mx(out=z_q[h][:].bitcast(FP8X4), scales=z_s[h][:], in_=z_bf[h][:])

        for h in range(2):
            for t in range(2):
                fetch_back(t, h)
        for t in range(2, PACK):
            fetch_back(t, 0)
        make_z(0)
        quant_z(0)

        z2 = sb("back0", [P, PACK, V], F32)
        for t in range(PACK):
            nc.vector.scalar_tensor_tensor(z2[:, t, :], b_ps[t][:], gb_half[:, t:t + 1], ds[t][:, 0:V],
                                           ALU.mult, ALU.add)
        far = [sb("ds%d" % t, [P, HALF], F32) for t in range(2, PACK)]
        for t in range(2, PACK):
            nc.scalar.activation(far[t - 2][:], st[t][:].indirect(n2_t[:, 16:32]), COPY)
        z2_bf = sb("z2_bf", [P, PACK * V], BF16)
        nc.vector.tensor_copy(out=z2_bf[:].rearrange("p (c i t) -> p c t i", i=4, t=PACK),
                              in_=z2[:].rearrange("p t (c i) -> p c t i", i=4))
        z2_q = sb("z2_q", [P, V], U32)
        z2_s = sb("z2_s", [P, V], U8)
        nc.vector.quantize_mx(out=z2_q[:].bitcast(FP8X4), scales=z2_s[:], in_=z2_bf[:])
        for t in range(2, PACK):
            nc.vector.tensor_tensor(back[1][:, t, :], far[t - 2][:], st[t][:, HALF:S], ALU.subtract)
        make_z(1)
        quant_z(1)

        for c in range(4):
            cols = slice((c % 2) * P, (c % 2 + 1) * P)
            s_ps = bank(1 + c, V)
            mx(s_ps[:], z_q[c // 2][:, cols], z_s[c // 2][:, cols], z2_q[:], z2_s[:])
            s_sb = sb("s_sb%d" % c, [P, V + SPARE], F32)
            nc.gpsimd.memset(s_sb[:, V:V + SPARE], 0.0)
            nc.scalar.activation(s_sb[:, 0:V], s_ps[:], COPY, scale=-0.0625)
            less = sb("less%d" % c, [P, V], F32)
            nc.scalar.activation(less[:], s_sb[:].indirect(n5_t[:]), COPY, scale=-1.0)
            res = sb("res%d" % c, [P, V], F32)
            nc.vector.tensor_tensor(res[:], s_sb[:].indirect(n4_t[:]), less[:], ALU.add)
            nc.sync.dma_start(out=out[c * P:(c + 1) * P, :], in_=res[:])
